import numpy as np
import ml_dtypes


def mxq(x, axis, fmt="e4m3"):
    dtype, down = {"e4m3": (ml_dtypes.float8_e4m3fn, 7), "e5m2": (ml_dtypes.float8_e5m2, 14)}[fmt]
    v = np.moveaxis(np.asarray(x, np.float32).astype(ml_dtypes.bfloat16).astype(np.float64), axis, -1)
    blocks = v.reshape(v.shape[:-1] + (-1, 32))
    amax = np.abs(blocks).max(-1, keepdims=True)
    byte = np.maximum(np.where(amax > 0, np.frexp(amax)[1] - 1 + 127, 0) - down, 1)
    scale = np.exp2(byte - 127.0)
    codes = (blocks / scale).astype(np.float32).astype(dtype).astype(np.float64)
    return np.moveaxis((codes * scale).reshape(v.shape), -1, axis)


WIDE = False


def mx_kscale(k):
    if not WIDE:
        return np.ones(k)
    levels = np.array([30, -30])
    if k % 512:
        return np.exp2(np.random.permutation(np.resize(levels, k // 32))).repeat(32)
    a = np.empty((k // 512, 16))
    for p in range(k // 512):
        a[p, :8] = np.random.permutation(np.resize(levels, 8))
        for g in range(8):
            far = levels[np.abs(levels - a[p, g]) >= 10]
            a[p, g + 8] = far[np.random.randint(len(far))]
    return np.exp2(a.ravel()).repeat(32)


def f64(x):
    return np.asarray(x).astype(np.float64)


def striped(idx):
    return np.tile(np.asarray(idx).reshape(-1, 16).T, (8, 1)).astype(np.uint16)


def unstriped(offs):
    return offs[:16].T.reshape(-1).astype(np.int64)


E2M1 = np.array([0.0, 0.5, 1.0, 1.5, 2.0, 3.0, 4.0, 6.0, -0.0, -0.5, -1.0, -1.5, -2.0, -3.0, -4.0, -6.0])


def pack_weight(w, fmt):
    k, n = w.shape
    w = f64(np.asarray(w, np.float32).astype(ml_dtypes.bfloat16)).reshape(k // 32, 32, n)
    amax = np.abs(w).max(1)
    if fmt in ("e4m3", "e5m2"):
        byte = np.frexp(amax)[1] - 1 + 127 - (7 if fmt == "e4m3" else 14)
    else:
        mant, ex = np.frexp(amax / 6.0)
        byte = np.where(mant > 0.5, ex, ex - 1) + 127
    byte = np.clip(np.where(amax > 0, byte, 1), 1, 254)
    scaled = (w * np.exp2(127.0 - byte)[:, None, :]).reshape(k, n).astype(np.float32)
    by_word = np.ascontiguousarray(scaled.reshape(k // 512, 128, 4, n).transpose(0, 1, 3, 2))
    if fmt in ("e4m3", "e5m2"):
        words = by_word.astype(ml_dtypes.float8_e4m3fn if fmt == "e4m3" else ml_dtypes.float8_e5m2).view(np.uint8)
    else:
        c = by_word.astype(ml_dtypes.float4_e2m1fn).view(np.uint8) & 0xF
        words = (c[..., 0::2] | (c[..., 1::2] << 4)).reshape(k // 512, 128, 2 * n)
    return np.ascontiguousarray(words), np.ascontiguousarray(byte.astype(np.uint8).reshape(k // 512, 16, n))


def unpack_weight(words, scales, fmt):
    g, _, n = scales.shape
    words = np.ascontiguousarray(words).reshape(g, 128, n, -1)
    if fmt in ("e4m3", "e5m2"):
        vals = words.view(ml_dtypes.float8_e4m3fn if fmt == "e4m3" else ml_dtypes.float8_e5m2).astype(np.float64)
    else:
        nib = np.empty((g, 128, n, 4), np.uint8)
        nib[..., 0::2] = words & 0xF
        nib[..., 1::2] = words >> 4
        vals = E2M1[nib]
    vals = vals * np.repeat(np.exp2(scales.astype(np.float64) - 127.0), 8, axis=1)[..., None]
    return vals.transpose(0, 1, 3, 2).reshape(g * 512, n)


def sigmoid(v):
    return 1.0 / (1.0 + np.exp(-v))


def bf(x):
    return np.asarray(x, np.float32).astype(ml_dtypes.bfloat16)


def planes(Y):
    r, m = Y.shape
    b = f64(bf(Y)).reshape(r // 32, 32, m)
    amax = np.abs(b).max(1)
    byte = np.clip(np.where(amax > 0, np.frexp(amax)[1] - 1 + 127 - 7, 1), 1, 254)
    codes = (b * np.exp2(127.0 - byte)[:, None, :]).reshape(r, m).astype(np.float32).astype(ml_dtypes.float8_e4m3fn).view(np.uint8)
    words = codes.reshape(r // 512, 128, 4, m).transpose(0, 1, 3, 2)
    return np.ascontiguousarray(words), np.ascontiguousarray(byte.astype(np.uint8).reshape(r // 512, 16, m))


K, T, J, R, F, Z, N = 512, 512, 256, 512, 512, 1024, 512


def setup_inputs():
    n = np.random.standard_normal
    idx = np.random.permutation(T)[:J]
    idx2 = np.random.permutation(Z)[:J]
    fk = mx_kscale(K)
    fr = mx_kscale(R)
    ff = mx_kscale(F)
    wp = pack_weight(n((K, R)) * 1 / np.sqrt(K) * fk[:, None] * fr, "e5m2")
    w2p = pack_weight(n((F, R)) * 1 / np.sqrt(F) * ff[:, None] * fr, "e5m2")
    wbp = pack_weight(n((R, N)) * 1 / np.sqrt(R) / fr[:, None], "e4m3")
    return {
        "xf": (n((K, T))).astype(np.float32),
        "fk": (np.random.uniform(0.5, 2.0, (K, 1)) / fk[:, None]).astype(np.float32),
        "w_words": wp[0],
        "w_scales": wp[1],
        "xo": (n((F, Z))).astype(np.float32),
        "fl": (np.random.uniform(0.5, 2.0, (F, 1)) / ff[:, None]).astype(np.float32),
        "so": (n((F, J))).astype(np.float32),
        "w2_words": w2p[0],
        "w2_scales": w2p[1],
        "wb_words": wbp[0],
        "wb_scales": wbp[1],
        "rs": (n((N, J))).astype(np.float32),
        "gm": (np.random.uniform(0.5, 2.0, (N, 1))).astype(np.float32),
        "offs": striped(idx),
        "offs2": striped(idx2),
    }


def reference(xf, fk, w_words, w_scales, xo, fl, so, w2_words, w2_scales, wb_words, wb_scales, rs, gm, offs, offs2):
    idx = unstriped(offs)
    idx2 = unstriped(offs2)
    wu = unpack_weight(w_words, w_scales, "e5m2")
    w2u = unpack_weight(w2_words, w2_scales, "e5m2")
    wbu = unpack_weight(wb_words, wb_scales, "e4m3")
    xg = f64(xf)[:, idx]
    x1 = np.pad(xg, ((0, 0), (1, 0)))[:, :J]
    u = (xg - 0.6 * x1) * f64(fk)
    u2 = f64(xo)[:, idx2] * sigmoid(f64(so)) * f64(fl)
    uq = mxq(u, 0, "e5m2")
    u2q = mxq(u2, 0, "e4m3")
    a = wu.T @ uq + w2u.T @ u2q
    ha = np.maximum(a, 0.0)
    h1 = np.pad(ha, ((0, 0), (2, 0)))[:, :J]
    hid = ha - 0.5 * h1
    hidq = mxq(hid, 0, "e5m2")
    p = wbu.T @ hidq
    y = f64(gm) * p + f64(rs)
    words, scales = planes(y)
    return y, words, scales

@@ -1,0 +1,212 @@
+from contextlib import ExitStack
+
+import concourse.mybir as mybir
+
+K, T, J, R, F, Z, N = 512, 512, 256, 512, 512, 1024, 512
+FLOPS = 2 * J * (K * R + F * R + R * N)
+
+F32 = mybir.dt.float32
+BF16 = mybir.dt.bfloat16
+I32 = mybir.dt.int32
+U32 = mybir.dt.uint32
+U16 = mybir.dt.uint16
+U8 = mybir.dt.uint8
+E4M3 = mybir.dt.float8_e4m3fn_x4
+E5M2 = mybir.dt.float8_e5m2_x4
+ALU = mybir.AluOpType
+ACT = mybir.ActivationFunctionType
+
+P = 128
+PACK = 4
+HALF = J // 2
+LIST_COLS = J // 16
+G_PAD = 8
+LAG = 2
+
+
+def tile_list_sum_steps_gated_lagged_residual_pl_kernel(
+    tc, xf, fk, w_words, w_scales, xo, fl, so, w2_words, w2_scales, wb_words, wb_scales,
+    rs, gm, offs, offs2, out_0, out_1, out_2,
+):
+    nc = tc.nc
+
+    def rows4(ap):
+        return ap.rearrange("(p t) c -> p t c", t=PACK)
+
+    def factor4(ap):
+        return ap.rearrange("(p t) o -> p (t o)", t=PACK)
+
+    def words_i32(ap):
+        return ap[0].rearrange("p c t -> p (c t)").bitcast(I32)
+
+    with ExitStack() as ctx:
+        sb = ctx.enter_context(tc.tile_pool(name="sb", bufs=1))
+        ps = ctx.enter_context(tc.psum_pool(name="ps", bufs=1))
+
+        offs_sb = sb.tile([P, LIST_COLS], U16, name="offs_sb")
+        offs2_sb = sb.tile([P, LIST_COLS], U16, name="offs2_sb")
+        sc_raw = sb.tile([P, 3, 512], U8, name="sc_raw", align_bytes=64)
+        sc = sb.tile([P, 3, PACK, P], U8, name="sc", align_bytes=64)
+        so_sb = sb.tile([P, PACK, J], F32, name="so_sb")
+        xf_sb = [sb.tile([P, 2, T], F32, name="xf_sb%d" % i) for i in range(2)]
+        xo_sb = [sb.tile([P, Z], F32, name="xo_sb%d" % t) for t in range(PACK)]
+        w_raw = [sb.tile([P, 512], U32, name="w_raw%d" % a) for a in range(3)]
+        w_sb = [sb.tile([P, PACK, P], U32, name="w_sb%d" % a, align_bytes=64) for a in range(3)]
+        rs_sb = sb.tile([P, PACK, J], F32, name="rs_sb")
+        fk_sb = sb.tile([P, PACK], F32, name="fk_sb")
+        fl_sb = sb.tile([P, PACK], F32, name="fl_sb")
+        gm_sb = sb.tile([P, PACK], F32, name="gm_sb")
+
+        xg = [sb.tile([P, G_PAD + J], F32, name="xg%d" % t) for t in range(PACK)]
+        step = [sb.tile([P, J], F32, name="step%d" % t) for t in range(PACK)]
+        u_pl = sb.tile([P, PACK, J], BF16, name="u_pl")
+        u_il = sb.tile([P, J, PACK], BF16, name="u_il", align_bytes=64)
+        u_q = sb.tile([P, J], U32, name="u_q", align_bytes=64)
+        u_s = sb.tile([P, J], U8, name="u_s", align_bytes=64)
+        gate = sb.tile([P, PACK, J], F32, name="gate")
+        og = [sb.tile([P, J], F32, name="og%d" % t) for t in range(PACK - 1)]
+        og_last = [sb.tile([P, HALF], F32, name="og_last%d" % h) for h in range(2)]
+        u2_pl = [sb.tile([P, PACK, HALF], BF16, name="u2_pl%d" % h) for h in range(2)]
+        ha = sb.tile([P, (LAG + J) * PACK], F32, name="ha")
+
+        nc.vector.memset(sc_raw[:].rearrange("p a c -> p (a c)").bitcast(I32), 0)
+        for t in range(PACK):
+            nc.vector.memset(xg[t][:, G_PAD - 1 : G_PAD], 0.0)
+        nc.vector.memset(ha[:, 0 : LAG * PACK], 0.0)
+
+        nc.sync.dma_start(offs_sb[:], offs)
+        nc.sync.dma_start(out=so_sb[:], in_=rows4(so))
+        for a, scales in enumerate((w_scales, w2_scales, wb_scales)):
+            nc.sync.dma_start(out=sc_raw[0:16, a, :].bitcast(I32), in_=scales[0].bitcast(I32))
+        for i in range(2):
+            nc.sync.dma_start(out=xf_sb[i][:], in_=rows4(xf)[:, 2 * i : 2 * i + 2, :])
+        nc.sync.dma_start(out=xo_sb[0][:], in_=rows4(xo)[:, 0, :])
+        nc.sync.dma_start(offs2_sb[:], offs2)
+        for t in range(1, PACK):
+            nc.sync.dma_start(out=xo_sb[t][:], in_=rows4(xo)[:, t, :])
+        for a, words in enumerate((w_words, w2_words, wb_words)):
+            nc.sync.dma_start(out=w_raw[a][:].bitcast(I32), in_=words_i32(words))
+        nc.sync.dma_start(out=rs_sb[:], in_=rows4(rs))
+        nc.gpsimd.dma_start(out=fk_sb[:], in_=factor4(fk))
+        nc.gpsimd.dma_start(out=fl_sb[:], in_=factor4(fl))
+        nc.gpsimd.dma_start(out=gm_sb[:], in_=factor4(gm))
+
+        nc.scalar.activation(gate[:], so_sb[:], ACT.Sigmoid)
+
+        nc.vector.tensor_copy(out=sc[:], in_=sc_raw[:].rearrange("p a (m t) -> p a t m", t=PACK))
+        sc_rows = sc[:].rearrange("p a t m -> p (a t m)").bitcast(I32)
+        for q in range(1, 4):
+            nc.gpsimd.dma_start(out=sc_rows[32 * q : 32 * q + 4, :], in_=sc_rows[4 * q : 4 * q + 4, :])
+
+        for t in range(PACK):
+            window = xf_sb[t // 2][:, t % 2, :].indirect(offs_sb[:])
+            if t == 2:
+                nc.vector.tensor_copy(xg[t][:, G_PAD:], window)
+            else:
+                nc.scalar.activation(xg[t][:, G_PAD:], window, ACT.Copy)
+        for t in range(PACK):
+            nc.vector.scalar_tensor_tensor(
+                out=step[t][:], in0=xg[t][:, G_PAD - 1 : G_PAD - 1 + J], scalar=-0.6,
+                in1=xg[t][:, G_PAD:], op0=ALU.mult, op1=ALU.add)
+        for t in range(PACK):
+            nc.vector.tensor_scalar(out=u_pl[:, t, :], in0=step[t][:], scalar1=fk_sb[:, t : t + 1],
+                                    scalar2=None, op0=ALU.mult)
+        nc.vector.tensor_copy(out=u_il[:], in_=u_pl[:].rearrange("p t j -> p j t"))
+        nc.vector.quantize_mx(out=u_q[:].bitcast(E5M2), scales=u_s[:],
+                              in_=u_il[:].rearrange("p j t -> p (j t)"))
+
+        for t in range(PACK - 1):
+            nc.scalar.activation(og[t][:], xo_sb[t][:].indirect(offs2_sb[:]), ACT.Copy)
+            for h in range(2):
+                cols = slice(h * HALF, (h + 1) * HALF)
+                nc.vector.scalar_tensor_tensor(
+                    out=u2_pl[h][:, t, :], in0=og[t][:, cols], scalar=fl_sb[:, t : t + 1],
+                    in1=gate[:, t, cols], op0=ALU.mult, op1=ALU.mult)
+        last = PACK - 1
+        half_list = LIST_COLS // 2
+        nc.vector.tensor_copy(og_last[0][:], xo_sb[last][:].indirect(offs2_sb[:, 0:half_list]))
+        nc.scalar.activation(og_last[1][:], xo_sb[last][:].indirect(offs2_sb[:, half_list:]), ACT.Copy)
+
+        def deal_words(a):
+            nc.scalar.copy(out=w_sb[a][:], in_=w_raw[a][:].rearrange("p (m t) -> p t m", t=PACK))
+
+        deal_words(0)
+        deal_words(1)
+
+        u2_il, u2_q, u2_s = [], [], []
+        for h in range(2):
+            cols = slice(h * HALF, (h + 1) * HALF)
+            nc.vector.scalar_tensor_tensor(
+                out=u2_pl[h][:, last, :], in0=og_last[h][:], scalar=fl_sb[:, last : last + 1],
+                in1=gate[:, last, cols], op0=ALU.mult, op1=ALU.mult)
+        for h in range(2):
+            il = sb.tile([P, HALF, PACK], BF16, name="u2_il%d" % h, align_bytes=64)
+            nc.vector.tensor_copy(out=il[:], in_=u2_pl[h][:].rearrange("p t j -> p j t"))
+            u2_il.append(il)
+        for h in range(2):
+            q_t = sb.tile([P, HALF], U32, name="u2_q%d" % h, align_bytes=64)
+            s_t = sb.tile([P, HALF], U8, name="u2_s%d" % h, align_bytes=64)
+            nc.vector.quantize_mx(out=q_t[:].bitcast(E4M3), scales=s_t[:],
+                                  in_=u2_il[h][:].rearrange("p j t -> p (j t)"))
+            u2_q.append(q_t)
+            u2_s.append(s_t)
+
+        acc_a = [ps.tile([P, PACK, HALF], F32, name="acc_a%d" % h) for h in range(2)]
+        for h in range(2):
+            cols = slice(h * HALF, (h + 1) * HALF)
+            for t in range(PACK):
+                nc.tensor.matmul_mx(out=acc_a[h][:, t, :], lhsT=w_sb[0][:, t, :].bitcast(E5M2),
+                                    lhsT_scale=sc[:, 0, t, :], rhs=u_q[:, cols].bitcast(E5M2),
+                                    rhs_scale=u_s[:, cols], start=(t == 0), stop=False)
+        for h in range(2):
+            for t in range(PACK):
+                nc.tensor.matmul_mx(out=acc_a[h][:, t, :], lhsT=w_sb[1][:, t, :].bitcast(E5M2),
+                                    lhsT_scale=sc[:, 1, t, :], rhs=u2_q[h][:].bitcast(E4M3),
+                                    rhs_scale=u2_s[h][:], start=False, stop=(t == PACK - 1))
+
+        deal_words(2)
+
+        W = HALF * PACK
+        hid_il, hid_q, hid_s = [], [], []
+        for h in range(2):
+            now = ha[:, LAG * PACK + h * W : LAG * PACK + (h + 1) * W]
+            nc.scalar.activation(now.rearrange("p (j t) -> p j t", t=PACK),
+                                 acc_a[h][:].rearrange("p t j -> p j t"), ACT.Relu)
+            il = sb.tile([P, W], BF16, name="hid_il%d" % h, align_bytes=64)
+            nc.vector.scalar_tensor_tensor(out=il[:], in0=ha[:, h * W : (h + 1) * W], scalar=-0.5,
+                                           in1=now, op0=ALU.mult, op1=ALU.add)
+            hid_il.append(il)
+        for h in range(2):
+            q_t = sb.tile([P, HALF], U32, name="hid_q%d" % h, align_bytes=64)
+            s_t = sb.tile([P, HALF], U8, name="hid_s%d" % h, align_bytes=64)
+            nc.vector.quantize_mx(out=q_t[:].bitcast(E5M2), scales=s_t[:], in_=hid_il[h][:])
+            hid_q.append(q_t)
+            hid_s.append(s_t)
+
+        y_q = sb.tile([P, J], U32, name="y_q", align_bytes=64)
+        y_s = sb.tile([P, J], U8, name="y_s", align_bytes=64)
+        y_il = []
+        for h in range(2):
+            cols = slice(h * HALF, (h + 1) * HALF)
+            acc_p = ps.tile([P, PACK, HALF], F32, name="acc_p%d" % h)
+            for t in range(PACK):
+                nc.tensor.matmul_mx(out=acc_p[:, t, :], lhsT=w_sb[2][:, t, :].bitcast(E4M3),
+                                    lhsT_scale=sc[:, 2, t, :], rhs=hid_q[h][:].bitcast(E5M2),
+                                    rhs_scale=hid_s[h][:], start=True, stop=True)
+            y = sb.tile([P, PACK, HALF], F32, name="y%d" % h)
+            for t in range(PACK):
+                nc.vector.scalar_tensor_tensor(out=y[:, t, :], in0=acc_p[:, t, :], scalar=gm_sb[:, t : t + 1],
+                                               in1=rs_sb[:, t, cols], op0=ALU.mult, op1=ALU.add)
+            nc.sync.dma_start(out=rows4(out_0)[:, :, cols], in_=y[:])
+            il = sb.tile([P, HALF, PACK], BF16, name="y_il%d" % h, align_bytes=64)
+            nc.scalar.copy(out=il[:], in_=y[:].rearrange("p t j -> p j t"))
+            y_il.append(il)
+        for h in range(2):
+            cols = slice(h * HALF, (h + 1) * HALF)
+            nc.vector.quantize_mx(out=y_q[:, cols].bitcast(E4M3), scales=y_s[:, cols],
+                                  in_=y_il[h][:].rearrange("p j t -> p (j t)"))
+            nc.sync.dma_start(out=words_i32(out_1)[:, cols], in_=y_q[:, cols].bitcast(I32))
+        for q in range(4):
+            queue = nc.scalar if q % 2 else nc.sync
+            queue.dma_start(out=out_2[0].bitcast(I32)[4 * q : 4 * q + 4, :],
+                            in_=y_s[32 * q : 32 * q + 4, :].bitcast(I32))

@@ -22,6 +22,7 @@ HALF = J // 2
 LIST_COLS = J // 16
 G_PAD = 8
 LAG = 2
+V_SPLIT = 56
 
 
 def tile_list_sum_steps_gated_lagged_residual_pl_kernel(
@@ -49,9 +50,9 @@ def tile_list_sum_steps_gated_lagged_residual_pl_kernel(
         sc = sb.tile([P, 3, PACK, P], U8, name="sc", align_bytes=64)
         so_sb = sb.tile([P, PACK, J], F32, name="so_sb")
         xf_sb = [sb.tile([P, 2, T], F32, name="xf_sb%d" % i) for i in range(2)]
-        xo_sb = [sb.tile([P, Z], F32, name="xo_sb%d" % t) for t in range(PACK)]
-        w_raw = [sb.tile([P, 512], U32, name="w_raw%d" % a) for a in range(3)]
-        w_sb = [sb.tile([P, PACK, P], U32, name="w_sb%d" % a, align_bytes=64) for a in range(3)]
+        xo_sb = [sb.tile([P, Z], F32, name="xo_sb%d" % t, tag="xo%d" % t, align_bytes=64) for t in range(PACK)]
+        w_raw = [sb.tile([P, 512], U32, name="w_raw%d" % a, tag="w_raw%d" % a, align_bytes=64) for a in range(3)]
+        w_sb = []
         rs_sb = sb.tile([P, PACK, J], F32, name="rs_sb")
         fk_sb = sb.tile([P, PACK], F32, name="fk_sb")
         fl_sb = sb.tile([P, PACK], F32, name="fl_sb")
@@ -60,13 +61,11 @@ def tile_list_sum_steps_gated_lagged_residual_pl_kernel(
         xg = [sb.tile([P, G_PAD + J], F32, name="xg%d" % t) for t in range(PACK)]
         step = [sb.tile([P, J], F32, name="step%d" % t) for t in range(PACK)]
         u_pl = sb.tile([P, PACK, J], BF16, name="u_pl")
-        u_il = sb.tile([P, J, PACK], BF16, name="u_il", align_bytes=64)
+        u_il = sb.tile([P, J, PACK], BF16, name="u_il", tag="u_il", align_bytes=64)
         u_q = sb.tile([P, J], U32, name="u_q", align_bytes=64)
         u_s = sb.tile([P, J], U8, name="u_s", align_bytes=64)
         gate = sb.tile([P, PACK, J], F32, name="gate")
-        og = [sb.tile([P, J], F32, name="og%d" % t) for t in range(PACK - 1)]
-        og_last = [sb.tile([P, HALF], F32, name="og_last%d" % h) for h in range(2)]
-        u2_pl = [sb.tile([P, PACK, HALF], BF16, name="u2_pl%d" % h) for h in range(2)]
+        og = [sb.tile([P, J], F32, name="og%d" % t, tag="og%d" % t) for t in range(PACK - 1)]
         ha = sb.tile([P, (LAG + J) * PACK], F32, name="ha")
 
         nc.vector.memset(sc_raw[:].rearrange("p a c -> p (a c)").bitcast(I32), 0)
@@ -76,19 +75,19 @@ def tile_list_sum_steps_gated_lagged_residual_pl_kernel(
 
         nc.sync.dma_start(offs_sb[:], offs)
         nc.sync.dma_start(out=so_sb[:], in_=rows4(so))
+        nc.sync.dma_start(out=fk_sb[:], in_=factor4(fk))
         for a, scales in enumerate((w_scales, w2_scales, wb_scales)):
             nc.sync.dma_start(out=sc_raw[0:16, a, :].bitcast(I32), in_=scales[0].bitcast(I32))
         for i in range(2):
             nc.sync.dma_start(out=xf_sb[i][:], in_=rows4(xf)[:, 2 * i : 2 * i + 2, :])
         nc.sync.dma_start(out=xo_sb[0][:], in_=rows4(xo)[:, 0, :])
         nc.sync.dma_start(offs2_sb[:], offs2)
+        nc.sync.dma_start(out=fl_sb[:], in_=factor4(fl))
         for t in range(1, PACK):
             nc.sync.dma_start(out=xo_sb[t][:], in_=rows4(xo)[:, t, :])
         for a, words in enumerate((w_words, w2_words, wb_words)):
             nc.sync.dma_start(out=w_raw[a][:].bitcast(I32), in_=words_i32(words))
         nc.sync.dma_start(out=rs_sb[:], in_=rows4(rs))
-        nc.gpsimd.dma_start(out=fk_sb[:], in_=factor4(fk))
-        nc.gpsimd.dma_start(out=fl_sb[:], in_=factor4(fl))
         nc.gpsimd.dma_start(out=gm_sb[:], in_=factor4(gm))
 
         nc.scalar.activation(gate[:], so_sb[:], ACT.Sigmoid)
@@ -115,6 +114,9 @@ def tile_list_sum_steps_gated_lagged_residual_pl_kernel(
         nc.vector.quantize_mx(out=u_q[:].bitcast(E5M2), scales=u_s[:],
                               in_=u_il[:].rearrange("p j t -> p (j t)"))
 
+        u2_both = sb.tile([P, 2 * PACK * HALF], BF16, name="u2_both", tag="u_il", align_bytes=64)
+        u2_pl = [u2_both[:, h * PACK * HALF : (h + 1) * PACK * HALF].rearrange("p (t j) -> p t j", t=PACK)
+                 for h in range(2)]
         for t in range(PACK - 1):
             nc.scalar.activation(og[t][:], xo_sb[t][:].indirect(offs2_sb[:]), ACT.Copy)
             for h in range(2):
@@ -124,11 +126,16 @@ def tile_list_sum_steps_gated_lagged_residual_pl_kernel(
                     in1=gate[:, t, cols], op0=ALU.mult, op1=ALU.mult)
         last = PACK - 1
         half_list = LIST_COLS // 2
+        og_last = [sb.tile([P, HALF], F32, name="og_last0", tag="og%d" % (last - 1)),
+                   sb.tile([P, HALF], F32, name="og_last1")]
         nc.vector.tensor_copy(og_last[0][:], xo_sb[last][:].indirect(offs2_sb[:, 0:half_list]))
         nc.scalar.activation(og_last[1][:], xo_sb[last][:].indirect(offs2_sb[:, half_list:]), ACT.Copy)
 
         def deal_words(a):
-            nc.scalar.copy(out=w_sb[a][:], in_=w_raw[a][:].rearrange("p (m t) -> p t m", t=PACK))
+            w_sb.append(sb.tile([P, PACK, P], U32, name="w_sb%d" % a, align_bytes=64,
+                                tag=("xo%d" % last, "w_raw0", "w_raw1")[a]))
+            nc.scalar.copy(out=w_sb[a][:].rearrange("p t m -> p m t"),
+                           in_=w_raw[a][:].rearrange("p (m t) -> p m t", t=PACK))
 
         deal_words(0)
         deal_words(1)
@@ -141,7 +148,7 @@ def tile_list_sum_steps_gated_lagged_residual_pl_kernel(
                 in1=gate[:, last, cols], op0=ALU.mult, op1=ALU.mult)
         for h in range(2):
             il = sb.tile([P, HALF, PACK], BF16, name="u2_il%d" % h, align_bytes=64)
-            nc.vector.tensor_copy(out=il[:], in_=u2_pl[h][:].rearrange("p t j -> p j t"))
+            nc.vector.tensor_copy(out=il[:], in_=u2_pl[h].rearrange("p t j -> p j t"))
             u2_il.append(il)
         for h in range(2):
             q_t = sb.tile([P, HALF], U32, name="u2_q%d" % h, align_bytes=64)
@@ -169,14 +176,18 @@ def tile_list_sum_steps_gated_lagged_residual_pl_kernel(
         W = HALF * PACK
         hid_il, hid_q, hid_s = [], [], []
         for h in range(2):
-            now = ha[:, LAG * PACK + h * W : LAG * PACK + (h + 1) * W]
-            nc.scalar.activation(now.rearrange("p (j t) -> p j t", t=PACK),
-                                 acc_a[h][:].rearrange("p t j -> p j t"), ACT.Relu)
             il = sb.tile([P, W], BF16, name="hid_il%d" % h, align_bytes=64)
-            nc.vector.scalar_tensor_tensor(out=il[:], in0=ha[:, h * W : (h + 1) * W], scalar=-0.5,
-                                           in1=now, op0=ALU.mult, op1=ALU.add)
+            for c in range(2):
+                lo = h * W + c * (W // 2)
+                now = ha[:, LAG * PACK + lo : LAG * PACK + lo + W // 2]
+                nc.scalar.activation(
+                    now.rearrange("p (j t) -> p j t", t=PACK),
+                    acc_a[h][:, :, c * (HALF // 2) : (c + 1) * (HALF // 2)].rearrange("p t j -> p j t"),
+                    ACT.Relu)
+                nc.vector.scalar_tensor_tensor(
+                    out=il[:, c * (W // 2) : (c + 1) * (W // 2)], in0=ha[:, lo : lo + W // 2], scalar=-0.5,
+                    in1=now, op0=ALU.mult, op1=ALU.add)
             hid_il.append(il)
-        for h in range(2):
             q_t = sb.tile([P, HALF], U32, name="hid_q%d" % h, align_bytes=64)
             s_t = sb.tile([P, HALF], U8, name="hid_s%d" % h, align_bytes=64)
             nc.vector.quantize_mx(out=q_t[:].bitcast(E5M2), scales=s_t[:], in_=hid_il[h][:])
@@ -188,18 +199,22 @@ def tile_list_sum_steps_gated_lagged_residual_pl_kernel(
         y_il = []
         for h in range(2):
             cols = slice(h * HALF, (h + 1) * HALF)
-            acc_p = ps.tile([P, PACK, HALF], F32, name="acc_p%d" % h)
+            acc_p = [ps.tile([P, 2, HALF], F32, name="acc_p%d%d" % (h, b)) for b in range(2)]
             for t in range(PACK):
-                nc.tensor.matmul_mx(out=acc_p[:, t, :], lhsT=w_sb[2][:, t, :].bitcast(E4M3),
+                nc.tensor.matmul_mx(out=acc_p[t // 2][:, t % 2, :], lhsT=w_sb[2][:, t, :].bitcast(E4M3),
                                     lhsT_scale=sc[:, 2, t, :], rhs=hid_q[h][:].bitcast(E5M2),
                                     rhs_scale=hid_s[h][:], start=True, stop=True)
             y = sb.tile([P, PACK, HALF], F32, name="y%d" % h)
             for t in range(PACK):
-                nc.vector.scalar_tensor_tensor(out=y[:, t, :], in0=acc_p[:, t, :], scalar=gm_sb[:, t : t + 1],
+                nc.vector.scalar_tensor_tensor(out=y[:, t, :], in0=acc_p[t // 2][:, t % 2, :], scalar=gm_sb[:, t : t + 1],
                                                in1=rs_sb[:, t, cols], op0=ALU.mult, op1=ALU.add)
             nc.sync.dma_start(out=rows4(out_0)[:, :, cols], in_=y[:])
             il = sb.tile([P, HALF, PACK], BF16, name="y_il%d" % h, align_bytes=64)
-            nc.scalar.copy(out=il[:], in_=y[:].rearrange("p t j -> p j t"))
+            by_scalar = HALF if h == 0 else V_SPLIT
+            nc.scalar.copy(out=il[:, 0:by_scalar, :], in_=y[:, :, 0:by_scalar].rearrange("p t j -> p j t"))
+            if by_scalar < HALF:
+                nc.vector.tensor_copy(out=il[:, by_scalar:, :],
+                                      in_=y[:, :, by_scalar:].rearrange("p t j -> p j t"))
             y_il.append(il)
         for h in range(2):
             cols = slice(h * HALF, (h + 1) * HALF)

@@ -46,10 +46,13 @@ def tile_list_sum_steps_gated_lagged_residual_pl_kernel(
 
         offs_sb = sb.tile([P, LIST_COLS], U16, name="offs_sb")
         offs2_sb = sb.tile([P, LIST_COLS], U16, name="offs2_sb")
-        sc_raw = sb.tile([P, 3, 512], U8, name="sc_raw", align_bytes=64)
-        sc = sb.tile([P, 3, PACK, P], U8, name="sc", align_bytes=64)
-        so_sb = sb.tile([P, PACK, J], F32, name="so_sb")
-        xf_sb = [sb.tile([P, 2, T], F32, name="xf_sb%d" % i) for i in range(2)]
+        sc_raw = sb.tile([P, 3 * 512], U8, name="sc_raw", align_bytes=64)
+        sc = []
+        so_first = sb.tile([P, J], F32, name="so_first")
+        so_rest = sb.tile([P, (PACK - 1) * J], F32, name="so_rest")
+        xf_one = [sb.tile([P, T], F32, name="xf_one%d" % t) for t in range(2)]
+        xf_two = sb.tile([P, 2 * T], F32, name="xf_two")
+        xf_sb = [xf_one[0][:], xf_one[1][:], xf_two[:, 0:T], xf_two[:, T:]]
         xo_sb = [sb.tile([P, Z], F32, name="xo_sb%d" % t, tag="xo%d" % t, align_bytes=64) for t in range(PACK)]
         w_raw = [sb.tile([P, 512], U32, name="w_raw%d" % a, tag="w_raw%d" % a, align_bytes=64) for a in range(3)]
         w_sb = []
@@ -60,73 +63,90 @@ def tile_list_sum_steps_gated_lagged_residual_pl_kernel(
 
         xg = [sb.tile([P, G_PAD + J], F32, name="xg%d" % t) for t in range(PACK)]
         step = [sb.tile([P, J], F32, name="step%d" % t) for t in range(PACK)]
-        u_pl = sb.tile([P, PACK, J], BF16, name="u_pl")
+        u_pl = sb.tile([P, PACK, J], BF16, name="u_pl", tag="u_pl", align_bytes=64)
         u_il = sb.tile([P, J, PACK], BF16, name="u_il", tag="u_il", align_bytes=64)
         u_q = sb.tile([P, J], U32, name="u_q", align_bytes=64)
         u_s = sb.tile([P, J], U8, name="u_s", align_bytes=64)
-        gate = sb.tile([P, PACK, J], F32, name="gate")
-        og = [sb.tile([P, J], F32, name="og%d" % t, tag="og%d" % t) for t in range(PACK - 1)]
+        gate_first = sb.tile([P, J], F32, name="gate_first")
+        gate_rest = sb.tile([P, (PACK - 1) * J], F32, name="gate_rest")
+        gate = [gate_first[:]] + [gate_rest[:, t * J : (t + 1) * J] for t in range(PACK - 1)]
+        og = [sb.tile([P, J], F32, name="og%d" % t, tag="og%d" % t, align_bytes=64) for t in range(PACK - 1)]
         ha = sb.tile([P, (LAG + J) * PACK], F32, name="ha")
 
-        nc.vector.memset(sc_raw[:].rearrange("p a c -> p (a c)").bitcast(I32), 0)
+        nc.gpsimd.memset(sc_raw[:].bitcast(I32), 0)
         for t in range(PACK):
             nc.vector.memset(xg[t][:, G_PAD - 1 : G_PAD], 0.0)
         nc.vector.memset(ha[:, 0 : LAG * PACK], 0.0)
 
+        def load_scales(a, q):
+            rows = (w_scales, w2_scales, wb_scales)[a][0].bitcast(I32)[4 * q : 4 * q + 4, :]
+            nc.sync.dma_start(out=sc_raw[32 * q : 32 * q + 4, 512 * a : 512 * (a + 1)].bitcast(I32), in_=rows)
+
+        def load_words(a):
+            nc.sync.dma_start(out=w_raw[a][:].bitcast(I32), in_=words_i32((w_words, w2_words, wb_words)[a]))
+
+        nc.sync.dma_start(out=xf_sb[0], in_=rows4(xf)[:, 0, :])
         nc.sync.dma_start(offs_sb[:], offs)
-        nc.sync.dma_start(out=so_sb[:], in_=rows4(so))
+        nc.sync.dma_start(out=so_first[:], in_=rows4(so)[:, 0, :])
         nc.sync.dma_start(out=fk_sb[:], in_=factor4(fk))
-        for a, scales in enumerate((w_scales, w2_scales, wb_scales)):
-            nc.sync.dma_start(out=sc_raw[0:16, a, :].bitcast(I32), in_=scales[0].bitcast(I32))
-        for i in range(2):
-            nc.sync.dma_start(out=xf_sb[i][:], in_=rows4(xf)[:, 2 * i : 2 * i + 2, :])
-        nc.sync.dma_start(out=xo_sb[0][:], in_=rows4(xo)[:, 0, :])
+        nc.sync.dma_start(out=xf_sb[1], in_=rows4(xf)[:, 1, :])
+        nc.sync.dma_start(out=xf_two[:].rearrange("p (t c) -> p t c", t=2), in_=rows4(xf)[:, 2:, :])
+        nc.sync.dma_start(out=so_rest[:].rearrange("p (t j) -> p t j", j=J), in_=rows4(so)[:, 1:, :])
         nc.sync.dma_start(offs2_sb[:], offs2)
-        nc.sync.dma_start(out=fl_sb[:], in_=factor4(fl))
-        for t in range(1, PACK):
+        for t in range(PACK):
+            if t == 2:
+                nc.sync.dma_start(out=fl_sb[:], in_=factor4(fl))
+            for q in range(2):
+                load_scales(t // 2, 2 * (t % 2) + q)
             nc.sync.dma_start(out=xo_sb[t][:], in_=rows4(xo)[:, t, :])
-        for a, words in enumerate((w_words, w2_words, wb_words)):
-            nc.sync.dma_start(out=w_raw[a][:].bitcast(I32), in_=words_i32(words))
+        load_words(0)
+        load_words(1)
+        for q in range(4):
+            load_scales(2, q)
+        load_words(2)
         nc.sync.dma_start(out=rs_sb[:], in_=rows4(rs))
-        nc.gpsimd.dma_start(out=gm_sb[:], in_=factor4(gm))
+        nc.sync.dma_start(out=gm_sb[:], in_=factor4(gm))
 
-        nc.scalar.activation(gate[:], so_sb[:], ACT.Sigmoid)
+        nc.scalar.activation(gate_first[:], so_first[:], ACT.Sigmoid)
 
-        nc.vector.tensor_copy(out=sc[:], in_=sc_raw[:].rearrange("p a (m t) -> p a t m", t=PACK))
-        sc_rows = sc[:].rearrange("p a t m -> p (a t m)").bitcast(I32)
-        for q in range(1, 4):
-            nc.gpsimd.dma_start(out=sc_rows[32 * q : 32 * q + 4, :], in_=sc_rows[4 * q : 4 * q + 4, :])
+        def deal_scales(a):
+            sc.append(sb.tile([P, PACK, P], U8, name="sc%d" % a, align_bytes=64,
+                              tag=("u_pl", "og1", "u2_il1")[a]))
+            nc.vector.tensor_copy(out=sc[a][:],
+                                  in_=sc_raw[:, 512 * a : 512 * (a + 1)].rearrange("p (m t) -> p t m", t=PACK))
 
         for t in range(PACK):
-            window = xf_sb[t // 2][:, t % 2, :].indirect(offs_sb[:])
-            if t == 2:
+            window = xf_sb[t].indirect(offs_sb[:])
+            if t == 0:
                 nc.vector.tensor_copy(xg[t][:, G_PAD:], window)
             else:
                 nc.scalar.activation(xg[t][:, G_PAD:], window, ACT.Copy)
-        for t in range(PACK):
             nc.vector.scalar_tensor_tensor(
                 out=step[t][:], in0=xg[t][:, G_PAD - 1 : G_PAD - 1 + J], scalar=-0.6,
                 in1=xg[t][:, G_PAD:], op0=ALU.mult, op1=ALU.add)
-        for t in range(PACK):
             nc.vector.tensor_scalar(out=u_pl[:, t, :], in0=step[t][:], scalar1=fk_sb[:, t : t + 1],
                                     scalar2=None, op0=ALU.mult)
+        nc.scalar.activation(gate_rest[:], so_rest[:], ACT.Sigmoid)
         nc.vector.tensor_copy(out=u_il[:], in_=u_pl[:].rearrange("p t j -> p j t"))
         nc.vector.quantize_mx(out=u_q[:].bitcast(E5M2), scales=u_s[:],
                               in_=u_il[:].rearrange("p j t -> p (j t)"))
+
+        deal_scales(0)
 
         u2_both = sb.tile([P, 2 * PACK * HALF], BF16, name="u2_both", tag="u_il", align_bytes=64)
         u2_pl = [u2_both[:, h * PACK * HALF : (h + 1) * PACK * HALF].rearrange("p (t j) -> p t j", t=PACK)
                  for h in range(2)]
         for t in range(PACK - 1):
             nc.scalar.activation(og[t][:], xo_sb[t][:].indirect(offs2_sb[:]), ACT.Copy)
-            for h in range(2):
-                cols = slice(h * HALF, (h + 1) * HALF)
-                nc.vector.scalar_tensor_tensor(
-                    out=u2_pl[h][:, t, :], in0=og[t][:, cols], scalar=fl_sb[:, t : t + 1],
-                    in1=gate[:, t, cols], op0=ALU.mult, op1=ALU.mult)
+            if t == PACK - 2:
+                deal_scales(1)
+            nc.vector.scalar_tensor_tensor(
+                out=u2_both[:].rearrange("p (h t j) -> p t h j", h=2, t=PACK)[:, t, :, :],
+                in0=og[t][:].rearrange("p (h j) -> p h j", h=2), scalar=fl_sb[:, t : t + 1],
+                in1=gate[t].rearrange("p (h j) -> p h j", h=2), op0=ALU.mult, op1=ALU.mult)
         last = PACK - 1
         half_list = LIST_COLS // 2
-        og_last = [sb.tile([P, HALF], F32, name="og_last0", tag="og%d" % (last - 1)),
+        og_last = [sb.tile([P, HALF], F32, name="og_last0", tag="og%d" % (last - 1), align_bytes=64),
                    sb.tile([P, HALF], F32, name="og_last1")]
         nc.vector.tensor_copy(og_last[0][:], xo_sb[last][:].indirect(offs2_sb[:, 0:half_list]))
         nc.scalar.activation(og_last[1][:], xo_sb[last][:].indirect(offs2_sb[:, half_list:]), ACT.Copy)
@@ -145,9 +165,9 @@ def tile_list_sum_steps_gated_lagged_residual_pl_kernel(
             cols = slice(h * HALF, (h + 1) * HALF)
             nc.vector.scalar_tensor_tensor(
                 out=u2_pl[h][:, last, :], in0=og_last[h][:], scalar=fl_sb[:, last : last + 1],
-                in1=gate[:, last, cols], op0=ALU.mult, op1=ALU.mult)
+                in1=gate[last][:, cols], op0=ALU.mult, op1=ALU.mult)
         for h in range(2):
-            il = sb.tile([P, HALF, PACK], BF16, name="u2_il%d" % h, align_bytes=64)
+            il = sb.tile([P, HALF, PACK], BF16, name="u2_il%d" % h, tag="u2_il%d" % h, align_bytes=64)
             nc.vector.tensor_copy(out=il[:], in_=u2_pl[h].rearrange("p t j -> p j t"))
             u2_il.append(il)
         for h in range(2):
@@ -163,15 +183,16 @@ def tile_list_sum_steps_gated_lagged_residual_pl_kernel(
             cols = slice(h * HALF, (h + 1) * HALF)
             for t in range(PACK):
                 nc.tensor.matmul_mx(out=acc_a[h][:, t, :], lhsT=w_sb[0][:, t, :].bitcast(E5M2),
-                                    lhsT_scale=sc[:, 0, t, :], rhs=u_q[:, cols].bitcast(E5M2),
+                                    lhsT_scale=sc[0][:, t, :], rhs=u_q[:, cols].bitcast(E5M2),
                                     rhs_scale=u_s[:, cols], start=(t == 0), stop=False)
         for h in range(2):
             for t in range(PACK):
                 nc.tensor.matmul_mx(out=acc_a[h][:, t, :], lhsT=w_sb[1][:, t, :].bitcast(E5M2),
-                                    lhsT_scale=sc[:, 1, t, :], rhs=u2_q[h][:].bitcast(E4M3),
+                                    lhsT_scale=sc[1][:, t, :], rhs=u2_q[h][:].bitcast(E4M3),
                                     rhs_scale=u2_s[h][:], start=False, stop=(t == PACK - 1))
 
         deal_words(2)
+        deal_scales(2)
 
         W = HALF * PACK
         hid_il, hid_q, hid_s = [], [], []
@@ -202,7 +223,7 @@ def tile_list_sum_steps_gated_lagged_residual_pl_kernel(
             acc_p = [ps.tile([P, 2, HALF], F32, name="acc_p%d%d" % (h, b)) for b in range(2)]
             for t in range(PACK):
                 nc.tensor.matmul_mx(out=acc_p[t // 2][:, t % 2, :], lhsT=w_sb[2][:, t, :].bitcast(E4M3),
-                                    lhsT_scale=sc[:, 2, t, :], rhs=hid_q[h][:].bitcast(E5M2),
+                                    lhsT_scale=sc[2][:, t, :], rhs=hid_q[h][:].bitcast(E5M2),
                                     rhs_scale=hid_s[h][:], start=True, stop=True)
             y = sb.tile([P, PACK, HALF], F32, name="y%d" % h)
             for t in range(PACK):

@@ -146,16 +146,19 @@ def tile_list_sum_steps_gated_lagged_residual_pl_kernel(
                 in1=gate[t].rearrange("p (h j) -> p h j", h=2), op0=ALU.mult, op1=ALU.mult)
         last = PACK - 1
         half_list = LIST_COLS // 2
-        og_last = [sb.tile([P, HALF], F32, name="og_last0", tag="og%d" % (last - 1), align_bytes=64),
-                   sb.tile([P, HALF], F32, name="og_last1")]
-        nc.vector.tensor_copy(og_last[0][:], xo_sb[last][:].indirect(offs2_sb[:, 0:half_list]))
-        nc.scalar.activation(og_last[1][:], xo_sb[last][:].indirect(offs2_sb[:, half_list:]), ACT.Copy)
+        og_last = [sb.tile([P, HALF], F32, name="og_last0"),
+                   sb.tile([P, HALF], F32, name="og_last1", tag="og%d" % (last - 1), align_bytes=64)]
+        nc.scalar.activation(og_last[0][:], xo_sb[last][:].indirect(offs2_sb[:, 0:half_list]), ACT.Copy)
+        nc.vector.tensor_copy(og_last[1][:], xo_sb[last][:].indirect(offs2_sb[:, half_list:]))
 
         def deal_words(a):
             w_sb.append(sb.tile([P, PACK, P], U32, name="w_sb%d" % a, align_bytes=64,
                                 tag=("xo%d" % last, "w_raw0", "w_raw1")[a]))
-            nc.scalar.copy(out=w_sb[a][:].rearrange("p t m -> p m t"),
-                           in_=w_raw[a][:].rearrange("p (m t) -> p m t", t=PACK))
+            pieces = 2 if a == 0 else 1
+            for b in range(pieces):
+                ts = slice(b * PACK // pieces, (b + 1) * PACK // pieces)
+                nc.scalar.copy(out=w_sb[a][:, ts, :].rearrange("p t m -> p m t"),
+                               in_=w_raw[a][:].rearrange("p (m t) -> p m t", t=PACK)[:, :, ts])
 
         deal_words(0)
         deal_words(1)
@@ -179,9 +182,9 @@ def tile_list_sum_steps_gated_lagged_residual_pl_kernel(
             u2_s.append(s_t)
 
         acc_a = [ps.tile([P, PACK, HALF], F32, name="acc_a%d" % h) for h in range(2)]
-        for h in range(2):
+        for b, h in ((0, 0), (0, 1), (1, 0), (1, 1)):
             cols = slice(h * HALF, (h + 1) * HALF)
-            for t in range(PACK):
+            for t in (2 * b, 2 * b + 1):
                 nc.tensor.matmul_mx(out=acc_a[h][:, t, :], lhsT=w_sb[0][:, t, :].bitcast(E5M2),
                                     lhsT_scale=sc[0][:, t, :], rhs=u_q[:, cols].bitcast(E5M2),
                                     rhs_scale=u_s[:, cols], start=(t == 0), stop=False)

from contextlib import ExitStack

import concourse.mybir as mybir

K, T, J, R, F, Z, N = 512, 512, 256, 512, 512, 1024, 512
FLOPS = 2 * J * (K * R + F * R + R * N)

F32 = mybir.dt.float32
BF16 = mybir.dt.bfloat16
I32 = mybir.dt.int32
U32 = mybir.dt.uint32
U16 = mybir.dt.uint16
U8 = mybir.dt.uint8
E4M3 = mybir.dt.float8_e4m3fn_x4
E5M2 = mybir.dt.float8_e5m2_x4
ALU = mybir.AluOpType
ACT = mybir.ActivationFunctionType

P = 128
PACK = 4
HALF = J // 2
LIST_COLS = J // 16
G_PAD = 8
LAG = 2
V_SPLIT = 56


def tile_list_sum_steps_gated_lagged_residual_pl_kernel(
    tc, xf, fk, w_words, w_scales, xo, fl, so, w2_words, w2_scales, wb_words, wb_scales,
    rs, gm, offs, offs2, out_0, out_1, out_2,
):
    nc = tc.nc

    def rows4(ap):
        return ap.rearrange("(p t) c -> p t c", t=PACK)

    def factor4(ap):
        return ap.rearrange("(p t) o -> p (t o)", t=PACK)

    def words_i32(ap):
        return ap[0].rearrange("p c t -> p (c t)").bitcast(I32)

    with ExitStack() as ctx:
        sb = ctx.enter_context(tc.tile_pool(name="sb", bufs=1))
        ps = ctx.enter_context(tc.psum_pool(name="ps", bufs=1))

        offs_sb = sb.tile([P, LIST_COLS], U16, name="offs_sb")
        offs2_sb = sb.tile([P, LIST_COLS], U16, name="offs2_sb")
        sc_raw = sb.tile([P, 3 * 512], U8, name="sc_raw", align_bytes=64)
        sc = []
        so_first = sb.tile([P, J], F32, name="so_first")
        so_rest = sb.tile([P, (PACK - 1) * J], F32, name="so_rest")
        xf_one = [sb.tile([P, T], F32, name="xf_one%d" % t) for t in range(2)]
        xf_two = sb.tile([P, 2 * T], F32, name="xf_two")
        xf_sb = [xf_one[0][:], xf_one[1][:], xf_two[:, 0:T], xf_two[:, T:]]
        xo_sb = [sb.tile([P, Z], F32, name="xo_sb%d" % t, tag="xo%d" % t, align_bytes=64) for t in range(PACK)]
        w_raw = [sb.tile([P, 512], U32, name="w_raw%d" % a, tag="w_raw%d" % a, align_bytes=64) for a in range(3)]
        w_sb = []
        rs_sb = sb.tile([P, PACK, J], F32, name="rs_sb")
        fk_sb = sb.tile([P, PACK], F32, name="fk_sb")
        fl_sb = sb.tile([P, PACK], F32, name="fl_sb")
        gm_sb = sb.tile([P, PACK], F32, name="gm_sb")

        xg = [sb.tile([P, G_PAD + J], F32, name="xg%d" % t) for t in range(PACK)]
        step = [sb.tile([P, J], F32, name="step%d" % t) for t in range(PACK)]
        u_pl = sb.tile([P, PACK, J], BF16, name="u_pl", tag="u_pl", align_bytes=64)
        u_il = sb.tile([P, J, PACK], BF16, name="u_il", tag="u_il", align_bytes=64)
        u_q = sb.tile([P, J], U32, name="u_q", align_bytes=64)
        u_s = sb.tile([P, J], U8, name="u_s", align_bytes=64)
        gate_first = sb.tile([P, J], F32, name="gate_first")
        gate_rest = sb.tile([P, (PACK - 1) * J], F32, name="gate_rest")
        gate = [gate_first[:]] + [gate_rest[:, t * J : (t + 1) * J] for t in range(PACK - 1)]
        og = [sb.tile([P, J], F32, name="og%d" % t, tag="og%d" % t, align_bytes=64) for t in range(PACK - 1)]
        ha = sb.tile([P, (LAG + J) * PACK], F32, name="ha")

        nc.gpsimd.memset(sc_raw[:].bitcast(I32), 0)
        for t in range(PACK):
            nc.vector.memset(xg[t][:, G_PAD - 1 : G_PAD], 0.0)
        nc.vector.memset(ha[:, 0 : LAG * PACK], 0.0)

        def load_scales(a, q):
            rows = (w_scales, w2_scales, wb_scales)[a][0].bitcast(I32)[4 * q : 4 * q + 4, :]
            nc.sync.dma_start(out=sc_raw[32 * q : 32 * q + 4, 512 * a : 512 * (a + 1)].bitcast(I32), in_=rows)

        def load_words(a):
            nc.sync.dma_start(out=w_raw[a][:].bitcast(I32), in_=words_i32((w_words, w2_words, wb_words)[a]))

        nc.sync.dma_start(out=xf_sb[0], in_=rows4(xf)[:, 0, :])
        nc.sync.dma_start(offs_sb[:], offs)
        nc.sync.dma_start(out=so_first[:], in_=rows4(so)[:, 0, :])
        nc.sync.dma_start(out=fk_sb[:], in_=factor4(fk))
        nc.sync.dma_start(out=xf_sb[1], in_=rows4(xf)[:, 1, :])
        nc.sync.dma_start(out=xf_two[:].rearrange("p (t c) -> p t c", t=2), in_=rows4(xf)[:, 2:, :])
        nc.sync.dma_start(out=so_rest[:].rearrange("p (t j) -> p t j", j=J), in_=rows4(so)[:, 1:, :])
        nc.sync.dma_start(offs2_sb[:], offs2)
        for t in range(PACK):
            if t == 2:
                nc.sync.dma_start(out=fl_sb[:], in_=factor4(fl))
            for q in range(2):
                load_scales(t // 2, 2 * (t % 2) + q)
            nc.sync.dma_start(out=xo_sb[t][:], in_=rows4(xo)[:, t, :])
        load_words(0)
        load_words(1)
        for q in range(4):
            load_scales(2, q)
        load_words(2)
        nc.sync.dma_start(out=rs_sb[:], in_=rows4(rs))
        nc.sync.dma_start(out=gm_sb[:], in_=factor4(gm))

        nc.scalar.activation(gate_first[:], so_first[:], ACT.Sigmoid)

        def deal_scales(a):
            sc.append(sb.tile([P, PACK, P], U8, name="sc%d" % a, align_bytes=64,
                              tag=("u_pl", "og1", "u2_il1")[a]))
            nc.vector.tensor_copy(out=sc[a][:],
                                  in_=sc_raw[:, 512 * a : 512 * (a + 1)].rearrange("p (m t) -> p t m", t=PACK))

        for t in range(PACK):
            window = xf_sb[t].indirect(offs_sb[:])
            if t == 0:
                nc.vector.tensor_copy(xg[t][:, G_PAD:], window)
            else:
                nc.scalar.activation(xg[t][:, G_PAD:], window, ACT.Copy)
            nc.vector.scalar_tensor_tensor(
                out=step[t][:], in0=xg[t][:, G_PAD - 1 : G_PAD - 1 + J], scalar=-0.6,
                in1=xg[t][:, G_PAD:], op0=ALU.mult, op1=ALU.add)
            nc.vector.tensor_scalar(out=u_pl[:, t, :], in0=step[t][:], scalar1=fk_sb[:, t : t + 1],
                                    scalar2=None, op0=ALU.mult)
        nc.scalar.activation(gate_rest[:], so_rest[:], ACT.Sigmoid)
        nc.vector.tensor_copy(out=u_il[:], in_=u_pl[:].rearrange("p t j -> p j t"))
        nc.vector.quantize_mx(out=u_q[:].bitcast(E5M2), scales=u_s[:],
                              in_=u_il[:].rearrange("p j t -> p (j t)"))

        deal_scales(0)

        u2_both = sb.tile([P, 2 * PACK * HALF], BF16, name="u2_both", tag="u_il", align_bytes=64)
        u2_pl = [u2_both[:, h * PACK * HALF : (h + 1) * PACK * HALF].rearrange("p (t j) -> p t j", t=PACK)
                 for h in range(2)]
        for t in range(PACK - 1):
            nc.scalar.activation(og[t][:], xo_sb[t][:].indirect(offs2_sb[:]), ACT.Copy)
            if t == PACK - 2:
                deal_scales(1)
            nc.vector.scalar_tensor_tensor(
                out=u2_both[:].rearrange("p (h t j) -> p t h j", h=2, t=PACK)[:, t, :, :],
                in0=og[t][:].rearrange("p (h j) -> p h j", h=2), scalar=fl_sb[:, t : t + 1],
                in1=gate[t].rearrange("p (h j) -> p h j", h=2), op0=ALU.mult, op1=ALU.mult)
        last = PACK - 1
        half_list = LIST_COLS // 2
        og_last = [sb.tile([P, HALF], F32, name="og_last0"),
                   sb.tile([P, HALF], F32, name="og_last1", tag="og%d" % (last - 1), align_bytes=64)]
        nc.scalar.activation(og_last[0][:], xo_sb[last][:].indirect(offs2_sb[:, 0:half_list]), ACT.Copy)
        nc.vector.tensor_copy(og_last[1][:], xo_sb[last][:].indirect(offs2_sb[:, half_list:]))

        def deal_words(a):
            w_sb.append(sb.tile([P, PACK, P], U32, name="w_sb%d" % a, align_bytes=64,
                                tag=("xo%d" % last, "w_raw0", "w_raw1")[a]))
            pieces = 2 if a == 0 else 1
            for b in range(pieces):
                ts = slice(b * PACK // pieces, (b + 1) * PACK // pieces)
                nc.scalar.copy(out=w_sb[a][:, ts, :].rearrange("p t m -> p m t"),
                               in_=w_raw[a][:].rearrange("p (m t) -> p m t", t=PACK)[:, :, ts])

        deal_words(0)
        deal_words(1)

        u2_il, u2_q, u2_s = [], [], []
        for h in range(2):
            cols = slice(h * HALF, (h + 1) * HALF)
            nc.vector.scalar_tensor_tensor(
                out=u2_pl[h][:, last, :], in0=og_last[h][:], scalar=fl_sb[:, last : last + 1],
                in1=gate[last][:, cols], op0=ALU.mult, op1=ALU.mult)
        for h in range(2):
            il = sb.tile([P, HALF, PACK], BF16, name="u2_il%d" % h, tag="u2_il%d" % h, align_bytes=64)
            nc.vector.tensor_copy(out=il[:], in_=u2_pl[h].rearrange("p t j -> p j t"))
            u2_il.append(il)
        for h in range(2):
            q_t = sb.tile([P, HALF], U32, name="u2_q%d" % h, align_bytes=64)
            s_t = sb.tile([P, HALF], U8, name="u2_s%d" % h, align_bytes=64)
            nc.vector.quantize_mx(out=q_t[:].bitcast(E4M3), scales=s_t[:],
                                  in_=u2_il[h][:].rearrange("p j t -> p (j t)"))
            u2_q.append(q_t)
            u2_s.append(s_t)

        acc_a = [ps.tile([P, PACK, HALF], F32, name="acc_a%d" % h) for h in range(2)]
        for b, h in ((0, 0), (0, 1), (1, 0), (1, 1)):
            cols = slice(h * HALF, (h + 1) * HALF)
            for t in (2 * b, 2 * b + 1):
                nc.tensor.matmul_mx(out=acc_a[h][:, t, :], lhsT=w_sb[0][:, t, :].bitcast(E5M2),
                                    lhsT_scale=sc[0][:, t, :], rhs=u_q[:, cols].bitcast(E5M2),
                                    rhs_scale=u_s[:, cols], start=(t == 0), stop=False)
        for h in range(2):
            for t in range(PACK):
                nc.tensor.matmul_mx(out=acc_a[h][:, t, :], lhsT=w_sb[1][:, t, :].bitcast(E5M2),
                                    lhsT_scale=sc[1][:, t, :], rhs=u2_q[h][:].bitcast(E4M3),
                                    rhs_scale=u2_s[h][:], start=False, stop=(t == PACK - 1))

        deal_words(2)
        deal_scales(2)

        W = HALF * PACK
        hid_il, hid_q, hid_s = [], [], []
        for h in range(2):
            il = sb.tile([P, W], BF16, name="hid_il%d" % h, align_bytes=64)
            for c in range(2):
                lo = h * W + c * (W // 2)
                now = ha[:, LAG * PACK + lo : LAG * PACK + lo + W // 2]
                nc.scalar.activation(
                    now.rearrange("p (j t) -> p j t", t=PACK),
                    acc_a[h][:, :, c * (HALF // 2) : (c + 1) * (HALF // 2)].rearrange("p t j -> p j t"),
                    ACT.Relu)
                nc.vector.scalar_tensor_tensor(
                    out=il[:, c * (W // 2) : (c + 1) * (W // 2)], in0=ha[:, lo : lo + W // 2], scalar=-0.5,
                    in1=now, op0=ALU.mult, op1=ALU.add)
            hid_il.append(il)
            q_t = sb.tile([P, HALF], U32, name="hid_q%d" % h, align_bytes=64)
            s_t = sb.tile([P, HALF], U8, name="hid_s%d" % h, align_bytes=64)
            nc.vector.quantize_mx(out=q_t[:].bitcast(E5M2), scales=s_t[:], in_=hid_il[h][:])
            hid_q.append(q_t)
            hid_s.append(s_t)

        y_q = sb.tile([P, J], U32, name="y_q", align_bytes=64)
        y_s = sb.tile([P, J], U8, name="y_s", align_bytes=64)
        y_il = []
        for h in range(2):
            cols = slice(h * HALF, (h + 1) * HALF)
            acc_p = [ps.tile([P, 2, HALF], F32, name="acc_p%d%d" % (h, b)) for b in range(2)]
            for t in range(PACK):
                nc.tensor.matmul_mx(out=acc_p[t // 2][:, t % 2, :], lhsT=w_sb[2][:, t, :].bitcast(E4M3),
                                    lhsT_scale=sc[2][:, t, :], rhs=hid_q[h][:].bitcast(E5M2),
                                    rhs_scale=hid_s[h][:], start=True, stop=True)
            y = sb.tile([P, PACK, HALF], F32, name="y%d" % h)
            for t in range(PACK):
                nc.vector.scalar_tensor_tensor(out=y[:, t, :], in0=acc_p[t // 2][:, t % 2, :], scalar=gm_sb[:, t : t + 1],
                                               in1=rs_sb[:, t, cols], op0=ALU.mult, op1=ALU.add)
            nc.sync.dma_start(out=rows4(out_0)[:, :, cols], in_=y[:])
            il = sb.tile([P, HALF, PACK], BF16, name="y_il%d" % h, align_bytes=64)
            by_scalar = HALF if h == 0 else V_SPLIT
            nc.scalar.copy(out=il[:, 0:by_scalar, :], in_=y[:, :, 0:by_scalar].rearrange("p t j -> p j t"))
            if by_scalar < HALF:
                nc.vector.tensor_copy(out=il[:, by_scalar:, :],
                                      in_=y[:, :, by_scalar:].rearrange("p t j -> p j t"))
            y_il.append(il)
        for h in range(2):
            cols = slice(h * HALF, (h + 1) * HALF)
            nc.vector.quantize_mx(out=y_q[:, cols].bitcast(E4M3), scales=y_s[:, cols],
                                  in_=y_il[h][:].rearrange("p j t -> p (j t)"))
            nc.sync.dma_start(out=words_i32(out_1)[:, cols], in_=y_q[:, cols].bitcast(I32))
        for q in range(4):
            queue = nc.scalar if q % 2 else nc.sync
            queue.dma_start(out=out_2[0].bitcast(I32)[4 * q : 4 * q + 4, :],
                            in_=y_s[32 * q : 32 * q + 4, :].bitcast(I32))
